import numpy as np
import ml_dtypes


def mxq(x, axis, fmt="e4m3"):
    dtype, down = {"e4m3": (ml_dtypes.float8_e4m3fn, 7), "e5m2": (ml_dtypes.float8_e5m2, 14)}[fmt]
    v = np.moveaxis(np.asarray(x, np.float32).astype(ml_dtypes.bfloat16).astype(np.float64), axis, -1)
    blocks = v.reshape(v.shape[:-1] + (-1, 32))
    amax = np.abs(blocks).max(-1, keepdims=True)
    byte = np.maximum(np.where(amax > 0, np.frexp(amax)[1] - 1 + 127, 0) - down, 1)
    scale = np.exp2(byte - 127.0)
    codes = (blocks / scale).astype(np.float32).astype(dtype).astype(np.float64)
    return np.moveaxis((codes * scale).reshape(v.shape), -1, axis)


WIDE = False


def mx_kscale(k):
    if not WIDE:
        return np.ones(k)
    levels = np.array([24, -24, 12, -12, 0])
    if k % 512:
        return np.exp2(np.random.permutation(np.resize(levels, k // 32))).repeat(32)
    a = np.empty((k // 512, 16))
    for p in range(k // 512):
        a[p, :8] = np.random.permutation(np.resize(levels, 8))
        for g in range(8):
            far = levels[np.abs(levels - a[p, g]) >= 10]
            a[p, g + 8] = far[np.random.randint(len(far))]
    return np.exp2(a.ravel()).repeat(32)


def f64(x):
    return np.asarray(x).astype(np.float64)


def striped8(idx):
    return np.concatenate([v.reshape(-1, 16).T for v in idx]).astype(np.uint16)


def unstriped8(offs):
    return np.stack([offs[16 * g:16 * g + 16].T.reshape(-1) for g in range(8)]).astype(np.int64)


E2M1 = np.array([0.0, 0.5, 1.0, 1.5, 2.0, 3.0, 4.0, 6.0, -0.0, -0.5, -1.0, -1.5, -2.0, -3.0, -4.0, -6.0])


def pack_weight(w, fmt):
    k, n = w.shape
    w = f64(np.asarray(w, np.float32).astype(ml_dtypes.bfloat16)).reshape(k // 32, 32, n)
    amax = np.abs(w).max(1)
    if fmt == "e4m3":
        byte = np.frexp(amax)[1] - 1 + 127 - 7
    else:
        mant, ex = np.frexp(amax / 6.0)
        byte = np.where(mant > 0.5, ex, ex - 1) + 127
    byte = np.clip(np.where(amax > 0, byte, 1), 1, 254)
    scaled = (w * np.exp2(127.0 - byte)[:, None, :]).reshape(k, n).astype(np.float32)
    by_word = np.ascontiguousarray(scaled.reshape(k // 512, 128, 4, n).transpose(0, 1, 3, 2))
    if fmt == "e4m3":
        words = by_word.astype(ml_dtypes.float8_e4m3fn).view(np.uint8)
    else:
        c = by_word.astype(ml_dtypes.float4_e2m1fn).view(np.uint8) & 0xF
        words = (c[..., 0::2] | (c[..., 1::2] << 4)).reshape(k // 512, 128, 2 * n)
    return np.ascontiguousarray(words), np.ascontiguousarray(byte.astype(np.uint8).reshape(k // 512, 16, n))


def unpack_weight(words, scales, fmt):
    g, _, n = scales.shape
    words = np.ascontiguousarray(words).reshape(g, 128, n, -1)
    if fmt == "e4m3":
        vals = words.view(ml_dtypes.float8_e4m3fn).astype(np.float64)
    else:
        nib = np.empty((g, 128, n, 4), np.uint8)
        nib[..., 0::2] = words & 0xF
        nib[..., 1::2] = words >> 4
        vals = E2M1[nib]
    vals = vals * np.repeat(np.exp2(scales.astype(np.float64) - 127.0), 8, axis=1)[..., None]
    return vals.transpose(0, 1, 3, 2).reshape(g * 512, n)


def sigm(f):
    return 1.0 / (1.0 + np.exp(-np.maximum(f, -700.0)))


K, N, T, J = 512, 512, 2048, 1024


def setup_inputs():
    n = np.random.standard_normal
    s = mx_kscale(K)[:, None]
    p_wv = pack_weight(n((K, N)) / np.sqrt(K) / s, "e4m3")
    return {
        "xT": (n((K, T)) * s).astype(np.float32),
        "wgt": np.repeat(np.random.uniform(0.5, 2.0, (8, J)), 16, axis=0).astype(np.float32),
        "wk": (n((K, N)) / np.sqrt(K) / s).astype(np.float32),
        "wv_words": p_wv[0],
        "wv_scales": p_wv[1],
        "bg": (0.3 * n(N) - 1.0).astype(np.float32),
        "res": (n((N, J))).astype(np.float32),
        "offs": striped8(np.stack([np.random.permutation(T)[:J] for _ in range(8)])),
    }


def reference(xT, wgt, wk, wv_words, wv_scales, bg, res, offs):
    idx = unstriped8(offs)
    rows = np.arange(K)
    xg = f64(wgt)[rows // 4 % 128] * f64(xT)[rows[:, None], idx[rows % 512 // 64]]
    xT_ = mxq(xg, 0, "e4m3")
    wk_ = mxq(f64(wk), 0, "e4m3")
    wv_ = unpack_weight(wv_words, wv_scales, "e4m3")
    ke = wk_.T @ xT_
    ve = wv_.T @ xT_
    gate = sigm(ke + f64(bg)[:, None])
    return f64(res) + gate * (np.maximum(ve, 0.0) - f64(res))

@@ -1,0 +1,215 @@
+from contextlib import ExitStack
+
+import concourse.mybir as mybir
+from concourse.masks import make_identity
+
+K, N, T, J = 512, 512, 2048, 1024
+FLOPS = 2 * 2 * K * N * J
+
+F32 = mybir.dt.float32
+BF16 = mybir.dt.bfloat16
+I32 = mybir.dt.int32
+U32 = mybir.dt.uint32
+U16 = mybir.dt.uint16
+U8 = mybir.dt.uint8
+FP8X4 = mybir.dt.float8_e4m3fn_x4
+ALU = mybir.AluOpType
+ACT = mybir.ActivationFunctionType
+
+P = 128
+PACK = 4
+HALF = 512
+CHUNK = 256
+LIST_ROWS = 16
+N_TILES = N // P
+VE_BANKS = 5
+KE_BANKS = 3
+
+
+def tile_list_hwayrelu_kernel(tc, xT, wgt, wk, wv_words, wv_scales, bg, res, offs, out):
+    nc = tc.nc
+    n_halves = J // HALF
+    n_chunks = J // CHUNK
+    chunks_per_half = HALF // CHUNK
+
+    with ExitStack() as ctx:
+        keep = ctx.enter_context(tc.tile_pool(name="keep", bufs=1))
+        ve_pool = ctx.enter_context(tc.psum_pool(name="ve", bufs=VE_BANKS))
+        ke_pool = ctx.enter_context(tc.psum_pool(name="ke", bufs=KE_BANKS))
+
+        offsets = keep.tile([P, J // LIST_ROWS], U16, name="offsets")
+        planes = [keep.tile([P, T], F32, name=f"plane{i}") for i in range(PACK)]
+        weights = [keep.tile([P, HALF], F32, name=f"weights{h}") for h in range(n_halves)]
+        wk_raw = [keep.tile([P, PACK, 2 * P], F32, name=f"wk_raw{u}") for u in range(2)]
+        wv_codes = keep.tile([P, N], U32, name="wv_codes", align_bytes=64)
+        wv_plane = keep.tile([P, N], U8, name="wv_plane", align_bytes=64)
+        bias_rows = keep.tile([P, P], F32, name="bias_rows")
+        identity = keep.tile([P, P], F32, name="identity")
+        neg_bias = keep.tile([P, N_TILES], F32, name="neg_bias")
+        warm = keep.tile([P, 1], F32, name="warm")
+        units = [(t, h) for t in range(N_TILES) for h in range(n_halves)]
+        res_first = [keep.tile([P, HALF], F32, name=f"res0_{h}") for h in range(n_halves)]
+        res_rest = [keep.tile([P, J], F32, name=f"res{t}") for t in range(1, N_TILES)]
+
+        x_planes = xT.rearrange("(p i) t -> i p t", i=PACK)
+        wk_view = wk.rearrange("(p i) n -> p i n", i=PACK)
+
+        nc.vector.memset(bias_rows[:], 0.0)
+        nc.vector.memset(wv_plane[:].bitcast(I32), 0)
+        nc.scalar.dma_start(out=bias_rows[0:N_TILES, :], in_=bg.rearrange("(t p) -> t p", p=P))
+        for q in range(4):
+            nc.scalar.dma_start(
+                out=wv_plane[32 * q : 32 * q + 4, :].bitcast(I32),
+                in_=wv_scales[0, 4 * q : 4 * q + 4, :].bitcast(I32),
+            )
+        nc.sync.dma_start(offsets[:], offs)
+        nc.sync.dma_start(out=weights[0][:], in_=wgt[:, 0:HALF])
+        nc.sync.dma_start(out=planes[0][:], in_=x_planes[0])
+        nc.sync.dma_start(out=weights[1][:], in_=wgt[:, HALF:J])
+        for i in range(1, PACK):
+            nc.sync.dma_start(out=planes[i][:], in_=x_planes[i])
+        nc.sync.dma_start(out=wk_raw[0][:], in_=wk_view[:, :, 0 : 2 * P])
+        nc.sync.dma_start(
+            out=wv_codes[:].bitcast(I32),
+            in_=wv_words[0].rearrange("p n i -> p (n i)").bitcast(I32),
+        )
+        nc.sync.dma_start(out=res_first[0][:], in_=res[0:P, 0:HALF])
+        nc.sync.dma_start(out=wk_raw[1][:], in_=wk_view[:, :, 2 * P : N])
+        nc.sync.dma_start(out=res_first[1][:], in_=res[0:P, HALF:J])
+        for t in range(1, N_TILES):
+            nc.sync.dma_start(out=res_rest[t - 1][:], in_=res[t * P : (t + 1) * P, :])
+
+        make_identity(nc, identity[:])
+        nc.scalar.activation(out=warm[:], in_=identity[:, 0:1], func=ACT.Sigmoid)
+        bias_bank = ke_pool.tile([P, HALF], F32, name="ke_bank")
+        nc.tensor.transpose(bias_bank[:, 0:P], bias_rows[:], identity[:])
+        nc.vector.tensor_scalar(
+            out=neg_bias[:], in0=bias_bank[:, 0:N_TILES], scalar1=-1.0, scalar2=None, op0=ALU.mult
+        )
+
+        picked_lo = [keep.tile([P, 2, HALF], F32, name=f"picked_lo{h}") for h in range(n_halves)]
+        picked_hi = [keep.tile([P, 2, CHUNK], F32, name=f"picked_hi{c}") for c in range(n_chunks)]
+        x_bf = [keep.tile([P, CHUNK, PACK], BF16, name=f"x_bf{c}", align_bytes=64) for c in range(n_chunks)]
+        x_codes = [keep.tile([P, HALF], U32, name=f"x_codes{h}", align_bytes=64) for h in range(n_halves)]
+        x_scales = [keep.tile([P, HALF], U8, name=f"x_scales{h}", align_bytes=64) for h in range(n_halves)]
+        wk_bf = [keep.tile([P, P, PACK], BF16, name=f"wk_bf{t}", align_bytes=64) for t in range(N_TILES)]
+        wk_codes = [keep.tile([P, P], U32, name=f"wk_codes{t}", align_bytes=64) for t in range(N_TILES)]
+        wk_scales = [keep.tile([P, P], U8, name=f"wk_scales{t}", align_bytes=64) for t in range(N_TILES)]
+
+        def gather(dst, i, j0, width):
+            h, c0 = divmod(j0, HALF)
+            listed = offsets[:, j0 // LIST_ROWS : (j0 + width) // LIST_ROWS]
+            nc.vector.tensor_tensor(dst, planes[i][:].indirect(listed), weights[h][:, c0 : c0 + width], ALU.mult)
+
+        def quantize_x(c):
+            h, cc = divmod(c, chunks_per_half)
+            cols = slice(cc * CHUNK, (cc + 1) * CHUNK)
+            nc.vector.quantize_mx(
+                out=x_codes[h][:, cols].bitcast(FP8X4),
+                scales=x_scales[h][:, cols],
+                in_=x_bf[c][:].rearrange("p j i -> p (j i)"),
+            )
+
+        def interleave_hi(c):
+            nc.scalar.copy(out=x_bf[c][:, :, 2:4], in_=picked_hi[c][:].rearrange("p i j -> p j i"))
+
+        def round_wk(t, on_vector):
+            src = wk_raw[t // 2][:, :, (t % 2) * P : (t % 2 + 1) * P].rearrange("p i (n e) -> p n i e", e=4)
+            dst = wk_bf[t][:].rearrange("p (n e) i -> p n i e", e=4)
+            if on_vector:
+                nc.vector.tensor_copy(out=dst, in_=src)
+            else:
+                nc.scalar.copy(out=dst, in_=src)
+
+        def quantize_wk(t):
+            nc.vector.quantize_mx(
+                out=wk_codes[t][:].bitcast(FP8X4),
+                scales=wk_scales[t][:],
+                in_=wk_bf[t][:].rearrange("p n i -> p (n i)"),
+            )
+
+        for i in range(2):
+            for h in range(n_halves):
+                gather(picked_lo[h][:, i, :], i, h * HALF, HALF)
+        for c in range(n_chunks):
+            h, cc = divmod(c, chunks_per_half)
+            nc.scalar.copy(
+                out=x_bf[c][:, :, 0:2],
+                in_=picked_lo[h][:, :, cc * CHUNK : (cc + 1) * CHUNK].rearrange("p i j -> p j i"),
+            )
+        for c in range(n_chunks):
+            gather(picked_hi[c][:, 0, :], 2, c * CHUNK, CHUNK)
+        for c in range(n_chunks):
+            gather(picked_hi[c][:, 1, :], 3, c * CHUNK, CHUNK)
+            interleave_hi(c)
+            if c >= 2:
+                quantize_x(c - 2)
+        round_wk(0, True)
+        quantize_x(n_chunks - 2)
+        quantize_wk(0)
+        quantize_x(n_chunks - 1)
+
+        ve_banks = {}
+        diffs = {}
+        gates = {}
+
+        def product(bank, codes, scales, h, width):
+            for j0 in range(0, HALF, width):
+                cols = slice(j0, j0 + width)
+                nc.tensor.matmul_mx(
+                    out=bank[:, cols],
+                    lhsT=codes.bitcast(FP8X4),
+                    lhsT_scale=scales,
+                    rhs=x_codes[h][:, cols].bitcast(FP8X4),
+                    rhs_scale=x_scales[h][:, cols],
+                    start=True,
+                    stop=True,
+                )
+
+        def front(u):
+            t, h = units[u]
+            width = CHUNK if t == 0 else HALF
+            rows = slice(t * P, (t + 1) * P)
+            ve_banks[u] = ve_pool.tile([P, HALF], F32, name="ve_bank")
+            product(ve_banks[u], wv_codes[:, rows], wv_plane[:, rows], h, width)
+            ke_bank = ke_pool.tile([P, HALF], F32, name="ke_bank")
+            product(ke_bank, wk_codes[t][:], wk_scales[t][:], h, width)
+            gates[u] = keep.tile([P, HALF], F32, name=f"gate{u}")
+            nc.scalar.activation(
+                out=gates[u][:], in_=ke_bank[:], func=ACT.Sigmoid, bias=neg_bias[:, t : t + 1], scale=-1.0
+            )
+            carried = res_first[h][:] if t == 0 else res_rest[t - 1][:, h * HALF : (h + 1) * HALF]
+            diffs[u] = keep.tile([P, HALF], F32, name=f"diff{u}")
+            nc.vector.scalar_tensor_tensor(
+                out=diffs[u][:], in0=ve_banks[u][:], scalar=0.0, in1=carried, op0=ALU.max, op1=ALU.subtract
+            )
+            nc.gpsimd.tensor_tensor(out=gates[u][:], in0=gates[u][:], in1=diffs[u][:], op=ALU.mult)
+
+        def back(u):
+            t, h = units[u]
+            width = CHUNK if u == len(units) - 1 else HALF
+            for j0 in range(0, HALF, width):
+                cols = slice(j0, j0 + width)
+                nc.vector.scalar_tensor_tensor(
+                    out=diffs[u][:, cols],
+                    in0=ve_banks[u][:, cols],
+                    scalar=0.0,
+                    in1=gates[u][:, cols],
+                    op0=ALU.max,
+                    op1=ALU.subtract,
+                )
+                nc.sync.dma_start(
+                    out=out[t * P : (t + 1) * P, h * HALF + j0 : h * HALF + j0 + width], in_=diffs[u][:, cols]
+                )
+
+        lead = 2
+        for u in range(len(units) + lead):
+            if u < len(units):
+                t, h = units[u]
+                if h == 0 and t + 1 < N_TILES:
+                    round_wk(t + 1, False)
+                front(u)
+                if h == 0 and t + 1 < N_TILES:
+                    quantize_wk(t + 1)
+            if u >= lead:
+                back(u - lead)

@@ -48,17 +48,20 @@ def tile_list_hwayrelu_kernel(tc, xT, wgt, wk, wv_words, wv_scales, bg, res, off
         neg_bias = keep.tile([P, N_TILES], F32, name="neg_bias")
         warm = keep.tile([P, 1], F32, name="warm")
         units = [(t, h) for t in range(N_TILES) for h in range(n_halves)]
-        res_first = [keep.tile([P, HALF], F32, name=f"res0_{h}") for h in range(n_halves)]
+        res_first = [keep.tile([P, HALF], F32, name=f"res0_{h}", tag=f"res0_{h}", align_bytes=64) for h in range(n_halves)]
         res_rest = [keep.tile([P, J], F32, name=f"res{t}") for t in range(1, N_TILES)]
 
         x_planes = xT.rearrange("(p i) t -> i p t", i=PACK)
         wk_view = wk.rearrange("(p i) n -> p i n", i=PACK)
 
+        wv_codes_zero = keep.tile([P, 1], F32, name="zero")
+        nc.vector.memset(wv_codes_zero[:], 0.0)
         nc.vector.memset(bias_rows[:], 0.0)
         nc.vector.memset(wv_plane[:].bitcast(I32), 0)
         nc.scalar.dma_start(out=bias_rows[0:N_TILES, :], in_=bg.rearrange("(t p) -> t p", p=P))
+        make_identity(nc, identity[:])
         for q in range(4):
-            nc.scalar.dma_start(
+            nc.gpsimd.dma_start(
                 out=wv_plane[32 * q : 32 * q + 4, :].bitcast(I32),
                 in_=wv_scales[0, 4 * q : 4 * q + 4, :].bitcast(I32),
             )
@@ -66,35 +69,33 @@ def tile_list_hwayrelu_kernel(tc, xT, wgt, wk, wv_words, wv_scales, bg, res, off
         nc.sync.dma_start(out=weights[0][:], in_=wgt[:, 0:HALF])
         nc.sync.dma_start(out=planes[0][:], in_=x_planes[0])
         nc.sync.dma_start(out=weights[1][:], in_=wgt[:, HALF:J])
-        for i in range(1, PACK):
-            nc.sync.dma_start(out=planes[i][:], in_=x_planes[i])
         nc.sync.dma_start(out=wk_raw[0][:], in_=wk_view[:, :, 0 : 2 * P])
+        nc.sync.dma_start(out=planes[1][:], in_=x_planes[1])
+        nc.sync.dma_start(out=planes[2][:], in_=x_planes[2])
+        nc.sync.dma_start(out=planes[3][:], in_=x_planes[3])
         nc.sync.dma_start(
             out=wv_codes[:].bitcast(I32),
             in_=wv_words[0].rearrange("p n i -> p (n i)").bitcast(I32),
         )
-        nc.sync.dma_start(out=res_first[0][:], in_=res[0:P, 0:HALF])
         nc.sync.dma_start(out=wk_raw[1][:], in_=wk_view[:, :, 2 * P : N])
+        nc.sync.dma_start(out=res_first[0][:], in_=res[0:P, 0:HALF])
         nc.sync.dma_start(out=res_first[1][:], in_=res[0:P, HALF:J])
         for t in range(1, N_TILES):
             nc.sync.dma_start(out=res_rest[t - 1][:], in_=res[t * P : (t + 1) * P, :])
 
-        make_identity(nc, identity[:])
-        nc.scalar.activation(out=warm[:], in_=identity[:, 0:1], func=ACT.Sigmoid)
+        nc.scalar.activation(out=warm[:], in_=wv_codes_zero[:, 0:1], func=ACT.Sigmoid)
         bias_bank = ke_pool.tile([P, HALF], F32, name="ke_bank")
         nc.tensor.transpose(bias_bank[:, 0:P], bias_rows[:], identity[:])
-        nc.vector.tensor_scalar(
-            out=neg_bias[:], in0=bias_bank[:, 0:N_TILES], scalar1=-1.0, scalar2=None, op0=ALU.mult
-        )
+        nc.scalar.activation(out=neg_bias[:], in_=bias_bank[:, 0:N_TILES], func=ACT.Copy, scale=-1.0)
 
         picked_lo = [keep.tile([P, 2, HALF], F32, name=f"picked_lo{h}") for h in range(n_halves)]
-        picked_hi = [keep.tile([P, 2, CHUNK], F32, name=f"picked_hi{c}") for c in range(n_chunks)]
+        picked_hi = [keep.tile([P, 2, HALF], F32, name=f"picked_hi{h}") for h in range(n_halves)]
         x_bf = [keep.tile([P, CHUNK, PACK], BF16, name=f"x_bf{c}", align_bytes=64) for c in range(n_chunks)]
         x_codes = [keep.tile([P, HALF], U32, name=f"x_codes{h}", align_bytes=64) for h in range(n_halves)]
         x_scales = [keep.tile([P, HALF], U8, name=f"x_scales{h}", align_bytes=64) for h in range(n_halves)]
-        wk_bf = [keep.tile([P, P, PACK], BF16, name=f"wk_bf{t}", align_bytes=64) for t in range(N_TILES)]
-        wk_codes = [keep.tile([P, P], U32, name=f"wk_codes{t}", align_bytes=64) for t in range(N_TILES)]
-        wk_scales = [keep.tile([P, P], U8, name=f"wk_scales{t}", align_bytes=64) for t in range(N_TILES)]
+        wk_bf = [keep.tile([P, 2 * P, PACK], BF16, name="wk_bf0", align_bytes=64)]
+        wk_codes = [keep.tile([P, 2 * P], U32, name=f"wk_codes{u}", align_bytes=64) for u in range(2)]
+        wk_scales = [keep.tile([P, 2 * P], U8, name=f"wk_scales{u}", align_bytes=64) for u in range(2)]
 
         def gather(dst, i, j0, width):
             h, c0 = divmod(j0, HALF)
@@ -111,42 +112,51 @@ def tile_list_hwayrelu_kernel(tc, xT, wgt, wk, wv_words, wv_scales, bg, res, off
             )
 
         def interleave_hi(c):
-            nc.scalar.copy(out=x_bf[c][:, :, 2:4], in_=picked_hi[c][:].rearrange("p i j -> p j i"))
-
-        def round_wk(t, on_vector):
-            src = wk_raw[t // 2][:, :, (t % 2) * P : (t % 2 + 1) * P].rearrange("p i (n e) -> p n i e", e=4)
-            dst = wk_bf[t][:].rearrange("p (n e) i -> p n i e", e=4)
-            if on_vector:
-                nc.vector.tensor_copy(out=dst, in_=src)
+            h, cc = divmod(c, chunks_per_half)
+            src = picked_hi[h][:, :, cc * CHUNK : (cc + 1) * CHUNK].rearrange("p i j -> p j i")
+            if c == n_chunks - 1:
+                nc.vector.tensor_copy(out=x_bf[c][:, :, 2:4], in_=src)
             else:
-                nc.scalar.copy(out=dst, in_=src)
+                nc.scalar.copy(out=x_bf[c][:, :, 2:4], in_=src)
 
-        def quantize_wk(t):
-            nc.vector.quantize_mx(
-                out=wk_codes[t][:].bitcast(FP8X4),
-                scales=wk_scales[t][:],
-                in_=wk_bf[t][:].rearrange("p n i -> p (n i)"),
+        def round_wk(t):
+            cols = slice((t % 2) * P, (t % 2 + 1) * P)
+            nc.scalar.copy(
+                out=wk_bf[t // 2][:, cols, :].rearrange("p (n e) i -> p n i e", e=4),
+                in_=wk_raw[t // 2][:, :, cols].rearrange("p i (n e) -> p n i e", e=4),
             )
 
-        for i in range(2):
-            for h in range(n_halves):
-                gather(picked_lo[h][:, i, :], i, h * HALF, HALF)
+        def quantize_wk(pair):
+            nc.vector.quantize_mx(
+                out=wk_codes[pair][:].bitcast(FP8X4),
+                scales=wk_scales[pair][:],
+                in_=wk_bf[pair][:].rearrange("p n i -> p (n i)"),
+            )
+
+        for h in range(n_halves):
+            gather(picked_lo[h][:, 0, :], 0, h * HALF, HALF)
+        round_wk(0)
+        round_wk(1)
+        quantize_wk(0)
+        for h in range(n_halves):
+            gather(picked_lo[h][:, 1, :], 1, h * HALF, HALF)
         for c in range(n_chunks):
             h, cc = divmod(c, chunks_per_half)
             nc.scalar.copy(
                 out=x_bf[c][:, :, 0:2],
                 in_=picked_lo[h][:, :, cc * CHUNK : (cc + 1) * CHUNK].rearrange("p i j -> p j i"),
             )
+        for h in range(n_halves):
+            gather(picked_hi[h][:, 0, :], 2, h * HALF, HALF)
         for c in range(n_chunks):
-            gather(picked_hi[c][:, 0, :], 2, c * CHUNK, CHUNK)
-        for c in range(n_chunks):
-            gather(picked_hi[c][:, 1, :], 3, c * CHUNK, CHUNK)
-            interleave_hi(c)
+            h, cc = divmod(c, chunks_per_half)
+            gather(picked_hi[h][:, 1, cc * CHUNK : (cc + 1) * CHUNK], 3, c * CHUNK, CHUNK)
+            if c < n_chunks - 1:
+                interleave_hi(c)
             if c >= 2:
                 quantize_x(c - 2)
-        round_wk(0, True)
+        interleave_hi(n_chunks - 1)
         quantize_x(n_chunks - 2)
-        quantize_wk(0)
         quantize_x(n_chunks - 1)
 
         ve_banks = {}
@@ -166,6 +176,10 @@ def tile_list_hwayrelu_kernel(tc, xT, wgt, wk, wv_words, wv_scales, bg, res, off
                     stop=True,
                 )
 
+        def carried(u):
+            t, h = units[u]
+            return res_first[h][:] if t == 0 else res_rest[t - 1][:, h * HALF : (h + 1) * HALF]
+
         def front(u):
             t, h = units[u]
             width = CHUNK if t == 0 else HALF
@@ -173,25 +187,29 @@ def tile_list_hwayrelu_kernel(tc, xT, wgt, wk, wv_words, wv_scales, bg, res, off
             ve_banks[u] = ve_pool.tile([P, HALF], F32, name="ve_bank")
             product(ve_banks[u], wv_codes[:, rows], wv_plane[:, rows], h, width)
             ke_bank = ke_pool.tile([P, HALF], F32, name="ke_bank")
-            product(ke_bank, wk_codes[t][:], wk_scales[t][:], h, width)
+            pair_cols = slice((t % 2) * P, (t % 2 + 1) * P)
+            product(ke_bank, wk_codes[t // 2][:, pair_cols], wk_scales[t // 2][:, pair_cols], h, width)
             gates[u] = keep.tile([P, HALF], F32, name=f"gate{u}")
             nc.scalar.activation(
                 out=gates[u][:], in_=ke_bank[:], func=ACT.Sigmoid, bias=neg_bias[:, t : t + 1], scale=-1.0
             )
-            carried = res_first[h][:] if t == 0 else res_rest[t - 1][:, h * HALF : (h + 1) * HALF]
             diffs[u] = keep.tile([P, HALF], F32, name=f"diff{u}")
             nc.vector.scalar_tensor_tensor(
-                out=diffs[u][:], in0=ve_banks[u][:], scalar=0.0, in1=carried, op0=ALU.max, op1=ALU.subtract
+                out=diffs[u][:], in0=ve_banks[u][:], scalar=0.0, in1=carried(u), op0=ALU.max, op1=ALU.subtract
             )
-            nc.gpsimd.tensor_tensor(out=gates[u][:], in0=gates[u][:], in1=diffs[u][:], op=ALU.mult)
+
+        def middle(u):
+            engine = nc.vector if u in (4, 6) else nc.gpsimd
+            engine.tensor_tensor(out=gates[u][:], in0=gates[u][:], in1=diffs[u][:], op=ALU.mult)
 
         def back(u):
             t, h = units[u]
             width = CHUNK if u == len(units) - 1 else HALF
+            result = carried(u + 2) if u + 2 < len(units) else diffs[u][:]
             for j0 in range(0, HALF, width):
                 cols = slice(j0, j0 + width)
                 nc.vector.scalar_tensor_tensor(
-                    out=diffs[u][:, cols],
+                    out=result[:, cols],
                     in0=ve_banks[u][:, cols],
                     scalar=0.0,
                     in1=gates[u][:, cols],
@@ -199,17 +217,26 @@ def tile_list_hwayrelu_kernel(tc, xT, wgt, wk, wv_words, wv_scales, bg, res, off
                     op1=ALU.subtract,
                 )
                 nc.sync.dma_start(
-                    out=out[t * P : (t + 1) * P, h * HALF + j0 : h * HALF + j0 + width], in_=diffs[u][:, cols]
+                    out=out[t * P : (t + 1) * P, h * HALF + j0 : h * HALF + j0 + width], in_=result[:, cols]
                 )
 
-        lead = 2
-        for u in range(len(units) + lead):
-            if u < len(units):
-                t, h = units[u]
-                if h == 0 and t + 1 < N_TILES:
-                    round_wk(t + 1, False)
-                front(u)
-                if h == 0 and t + 1 < N_TILES:
-                    quantize_wk(t + 1)
-            if u >= lead:
-                back(u - lead)
+        front(0)
+        middle(0)
+        front(1)
+        middle(1)
+        wk_bf.append(keep.tile([P, 2 * P, PACK], BF16, name="wk_bf1", tag="res0_1", align_bytes=64))
+        round_wk(2)
+        front(2)
+        middle(2)
+        back(0)
+        round_wk(3)
+        front(3)
+        middle(3)
+        back(1)
+        quantize_wk(1)
+        for u in range(4, len(units)):
+            front(u)
+            middle(u)
+            back(u - 2)
+        back(len(units) - 2)
+        back(len(units) - 1)

@@ -69,16 +69,15 @@ def tile_list_hwayrelu_kernel(tc, xT, wgt, wk, wv_words, wv_scales, bg, res, off
         nc.sync.dma_start(out=weights[0][:], in_=wgt[:, 0:HALF])
         nc.sync.dma_start(out=planes[0][:], in_=x_planes[0])
         nc.sync.dma_start(out=weights[1][:], in_=wgt[:, HALF:J])
+        for i in range(1, PACK):
+            nc.sync.dma_start(out=planes[i][:], in_=x_planes[i])
         nc.sync.dma_start(out=wk_raw[0][:], in_=wk_view[:, :, 0 : 2 * P])
-        nc.sync.dma_start(out=planes[1][:], in_=x_planes[1])
-        nc.sync.dma_start(out=planes[2][:], in_=x_planes[2])
-        nc.sync.dma_start(out=planes[3][:], in_=x_planes[3])
         nc.sync.dma_start(
             out=wv_codes[:].bitcast(I32),
             in_=wv_words[0].rearrange("p n i -> p (n i)").bitcast(I32),
         )
-        nc.sync.dma_start(out=wk_raw[1][:], in_=wk_view[:, :, 2 * P : N])
         nc.sync.dma_start(out=res_first[0][:], in_=res[0:P, 0:HALF])
+        nc.sync.dma_start(out=wk_raw[1][:], in_=wk_view[:, :, 2 * P : N])
         nc.sync.dma_start(out=res_first[1][:], in_=res[0:P, HALF:J])
         for t in range(1, N_TILES):
             nc.sync.dma_start(out=res_rest[t - 1][:], in_=res[t * P : (t + 1) * P, :])
@@ -121,25 +120,24 @@ def tile_list_hwayrelu_kernel(tc, xT, wgt, wk, wv_words, wv_scales, bg, res, off
 
         def round_wk(t):
             cols = slice((t % 2) * P, (t % 2 + 1) * P)
-            nc.scalar.copy(
-                out=wk_bf[t // 2][:, cols, :].rearrange("p (n e) i -> p n i e", e=4),
-                in_=wk_raw[t // 2][:, :, cols].rearrange("p i (n e) -> p n i e", e=4),
-            )
+            dst = wk_bf[t // 2][:, cols, :].rearrange("p (n e) i -> p n i e", e=4)
+            src = wk_raw[t // 2][:, :, cols].rearrange("p i (n e) -> p n i e", e=4)
+            if t == 0:
+                nc.vector.tensor_copy(out=dst, in_=src)
+            else:
+                nc.scalar.copy(out=dst, in_=src)
 
-        def quantize_wk(pair):
+        def quantize_wk(t0, count):
+            cols = slice((t0 % 2) * P, (t0 % 2 + count) * P)
             nc.vector.quantize_mx(
-                out=wk_codes[pair][:].bitcast(FP8X4),
-                scales=wk_scales[pair][:],
-                in_=wk_bf[pair][:].rearrange("p n i -> p (n i)"),
+                out=wk_codes[t0 // 2][:, cols].bitcast(FP8X4),
+                scales=wk_scales[t0 // 2][:, cols],
+                in_=wk_bf[t0 // 2][:, cols, :].rearrange("p n i -> p (n i)"),
             )
 
-        for h in range(n_halves):
-            gather(picked_lo[h][:, 0, :], 0, h * HALF, HALF)
-        round_wk(0)
-        round_wk(1)
-        quantize_wk(0)
-        for h in range(n_halves):
-            gather(picked_lo[h][:, 1, :], 1, h * HALF, HALF)
+        for i in range(2):
+            for h in range(n_halves):
+                gather(picked_lo[h][:, i, :], i, h * HALF, HALF)
         for c in range(n_chunks):
             h, cc = divmod(c, chunks_per_half)
             nc.scalar.copy(
@@ -153,15 +151,20 @@ def tile_list_hwayrelu_kernel(tc, xT, wgt, wk, wv_words, wv_scales, bg, res, off
             gather(picked_hi[h][:, 1, cc * CHUNK : (cc + 1) * CHUNK], 3, c * CHUNK, CHUNK)
             if c < n_chunks - 1:
                 interleave_hi(c)
-            if c >= 2:
-                quantize_x(c - 2)
+        round_wk(0)
+        round_wk(1)
+        quantize_x(0)
+        quantize_wk(0, 1)
+        quantize_x(1)
         interleave_hi(n_chunks - 1)
-        quantize_x(n_chunks - 2)
-        quantize_x(n_chunks - 1)
+        quantize_x(2)
+        quantize_x(3)
+        quantize_wk(1, 1)
 
         ve_banks = {}
         diffs = {}
         gates = {}
+        gated = {}
 
         def product(bank, codes, scales, h, width):
             for j0 in range(0, HALF, width):
@@ -199,20 +202,31 @@ def tile_list_hwayrelu_kernel(tc, xT, wgt, wk, wv_words, wv_scales, bg, res, off
             )
 
         def middle(u):
-            engine = nc.vector if u in (4, 6) else nc.gpsimd
-            engine.tensor_tensor(out=gates[u][:], in0=gates[u][:], in1=diffs[u][:], op=ALU.mult)
+            if u == 4:
+                gated[u] = carried(6)
+            elif u == 7:
+                gated[u] = gates[5][:]
+            else:
+                gated[u] = gates[u][:]
+            engine = nc.vector if u in (4, 7) else nc.gpsimd
+            engine.tensor_tensor(out=gated[u], in0=gates[u][:], in1=diffs[u][:], op=ALU.mult)
 
         def back(u):
             t, h = units[u]
             width = CHUNK if u == len(units) - 1 else HALF
-            result = carried(u + 2) if u + 2 < len(units) else diffs[u][:]
+            if u in (3, 6):
+                result = gates[u + 1][:]
+            elif u == 7:
+                result = diffs[u][:]
+            else:
+                result = carried(u + 2)
             for j0 in range(0, HALF, width):
                 cols = slice(j0, j0 + width)
                 nc.vector.scalar_tensor_tensor(
                     out=result[:, cols],
                     in0=ve_banks[u][:, cols],
                     scalar=0.0,
-                    in1=gates[u][:, cols],
+                    in1=gated[u][:, cols],
                     op0=ALU.max,
                     op1=ALU.subtract,
                 )
@@ -233,10 +247,18 @@ def tile_list_hwayrelu_kernel(tc, xT, wgt, wk, wv_words, wv_scales, bg, res, off
         front(3)
         middle(3)
         back(1)
-        quantize_wk(1)
-        for u in range(4, len(units)):
-            front(u)
-            middle(u)
-            back(u - 2)
-        back(len(units) - 2)
-        back(len(units) - 1)
+        quantize_wk(2, 2)
+        front(4)
+        back(2)
+        front(5)
+        middle(5)
+        front(6)
+        middle(6)
+        middle(4)
+        back(3)
+        back(4)
+        front(7)
+        back(5)
+        middle(7)
+        back(6)
+        back(7)

@@ -164,7 +164,6 @@ def tile_list_hwayrelu_kernel(tc, xT, wgt, wk, wv_words, wv_scales, bg, res, off
         ve_banks = {}
         diffs = {}
         gates = {}
-        gated = {}
 
         def product(bank, codes, scales, h, width):
             for j0 in range(0, HALF, width):
@@ -202,31 +201,20 @@ def tile_list_hwayrelu_kernel(tc, xT, wgt, wk, wv_words, wv_scales, bg, res, off
             )
 
         def middle(u):
-            if u == 4:
-                gated[u] = carried(6)
-            elif u == 7:
-                gated[u] = gates[5][:]
-            else:
-                gated[u] = gates[u][:]
-            engine = nc.vector if u in (4, 7) else nc.gpsimd
-            engine.tensor_tensor(out=gated[u], in0=gates[u][:], in1=diffs[u][:], op=ALU.mult)
+            engine = nc.vector if u in (4, 6) else nc.gpsimd
+            engine.tensor_tensor(out=gates[u][:], in0=gates[u][:], in1=diffs[u][:], op=ALU.mult)
 
         def back(u):
             t, h = units[u]
             width = CHUNK if u == len(units) - 1 else HALF
-            if u in (3, 6):
-                result = gates[u + 1][:]
-            elif u == 7:
-                result = diffs[u][:]
-            else:
-                result = carried(u + 2)
+            result = carried(u + 2) if u + 2 < len(units) else diffs[u][:]
             for j0 in range(0, HALF, width):
                 cols = slice(j0, j0 + width)
                 nc.vector.scalar_tensor_tensor(
                     out=result[:, cols],
                     in0=ve_banks[u][:, cols],
                     scalar=0.0,
-                    in1=gated[u][:, cols],
+                    in1=gates[u][:, cols],
                     op0=ALU.max,
                     op1=ALU.subtract,
                 )
@@ -248,17 +236,9 @@ def tile_list_hwayrelu_kernel(tc, xT, wgt, wk, wv_words, wv_scales, bg, res, off
         middle(3)
         back(1)
         quantize_wk(2, 2)
-        front(4)
-        back(2)
-        front(5)
-        middle(5)
-        front(6)
-        middle(6)
-        middle(4)
-        back(3)
-        back(4)
-        front(7)
-        back(5)
-        middle(7)
-        back(6)
-        back(7)
+        for u in range(4, len(units)):
+            front(u)
+            middle(u)
+            back(u - 2)
+        back(len(units) - 2)
+        back(len(units) - 1)

from contextlib import ExitStack

import concourse.mybir as mybir
from concourse.masks import make_identity

K, N, T, J = 512, 512, 2048, 1024
FLOPS = 2 * 2 * K * N * J

F32 = mybir.dt.float32
BF16 = mybir.dt.bfloat16
I32 = mybir.dt.int32
U32 = mybir.dt.uint32
U16 = mybir.dt.uint16
U8 = mybir.dt.uint8
FP8X4 = mybir.dt.float8_e4m3fn_x4
ALU = mybir.AluOpType
ACT = mybir.ActivationFunctionType

P = 128
PACK = 4
HALF = 512
CHUNK = 256
LIST_ROWS = 16
N_TILES = N // P
VE_BANKS = 5
KE_BANKS = 3


def tile_list_hwayrelu_kernel(tc, xT, wgt, wk, wv_words, wv_scales, bg, res, offs, out):
    nc = tc.nc
    n_halves = J // HALF
    n_chunks = J // CHUNK
    chunks_per_half = HALF // CHUNK

    with ExitStack() as ctx:
        keep = ctx.enter_context(tc.tile_pool(name="keep", bufs=1))
        ve_pool = ctx.enter_context(tc.psum_pool(name="ve", bufs=VE_BANKS))
        ke_pool = ctx.enter_context(tc.psum_pool(name="ke", bufs=KE_BANKS))

        offsets = keep.tile([P, J // LIST_ROWS], U16, name="offsets")
        planes = [keep.tile([P, T], F32, name=f"plane{i}") for i in range(PACK)]
        weights = [keep.tile([P, HALF], F32, name=f"weights{h}") for h in range(n_halves)]
        wk_raw = [keep.tile([P, PACK, 2 * P], F32, name=f"wk_raw{u}") for u in range(2)]
        wv_codes = keep.tile([P, N], U32, name="wv_codes", align_bytes=64)
        wv_plane = keep.tile([P, N], U8, name="wv_plane", align_bytes=64)
        bias_rows = keep.tile([P, P], F32, name="bias_rows")
        identity = keep.tile([P, P], F32, name="identity")
        neg_bias = keep.tile([P, N_TILES], F32, name="neg_bias")
        warm = keep.tile([P, 1], F32, name="warm")
        units = [(t, h) for t in range(N_TILES) for h in range(n_halves)]
        res_first = [keep.tile([P, HALF], F32, name=f"res0_{h}", tag=f"res0_{h}", align_bytes=64) for h in range(n_halves)]
        res_rest = [keep.tile([P, J], F32, name=f"res{t}") for t in range(1, N_TILES)]

        x_planes = xT.rearrange("(p i) t -> i p t", i=PACK)
        wk_view = wk.rearrange("(p i) n -> p i n", i=PACK)

        wv_codes_zero = keep.tile([P, 1], F32, name="zero")
        nc.vector.memset(wv_codes_zero[:], 0.0)
        nc.vector.memset(bias_rows[:], 0.0)
        nc.vector.memset(wv_plane[:].bitcast(I32), 0)
        nc.scalar.dma_start(out=bias_rows[0:N_TILES, :], in_=bg.rearrange("(t p) -> t p", p=P))
        make_identity(nc, identity[:])
        for q in range(4):
            nc.gpsimd.dma_start(
                out=wv_plane[32 * q : 32 * q + 4, :].bitcast(I32),
                in_=wv_scales[0, 4 * q : 4 * q + 4, :].bitcast(I32),
            )
        nc.sync.dma_start(offsets[:], offs)
        nc.sync.dma_start(out=weights[0][:], in_=wgt[:, 0:HALF])
        nc.sync.dma_start(out=planes[0][:], in_=x_planes[0])
        nc.sync.dma_start(out=weights[1][:], in_=wgt[:, HALF:J])
        for i in range(1, PACK):
            nc.sync.dma_start(out=planes[i][:], in_=x_planes[i])
        nc.sync.dma_start(out=wk_raw[0][:], in_=wk_view[:, :, 0 : 2 * P])
        nc.sync.dma_start(
            out=wv_codes[:].bitcast(I32),
            in_=wv_words[0].rearrange("p n i -> p (n i)").bitcast(I32),
        )
        nc.sync.dma_start(out=res_first[0][:], in_=res[0:P, 0:HALF])
        nc.sync.dma_start(out=wk_raw[1][:], in_=wk_view[:, :, 2 * P : N])
        nc.sync.dma_start(out=res_first[1][:], in_=res[0:P, HALF:J])
        for t in range(1, N_TILES):
            nc.sync.dma_start(out=res_rest[t - 1][:], in_=res[t * P : (t + 1) * P, :])

        nc.scalar.activation(out=warm[:], in_=wv_codes_zero[:, 0:1], func=ACT.Sigmoid)
        bias_bank = ke_pool.tile([P, HALF], F32, name="ke_bank")
        nc.tensor.transpose(bias_bank[:, 0:P], bias_rows[:], identity[:])
        nc.scalar.activation(out=neg_bias[:], in_=bias_bank[:, 0:N_TILES], func=ACT.Copy, scale=-1.0)

        picked_lo = [keep.tile([P, 2, HALF], F32, name=f"picked_lo{h}") for h in range(n_halves)]
        picked_hi = [keep.tile([P, 2, HALF], F32, name=f"picked_hi{h}") for h in range(n_halves)]
        x_bf = [keep.tile([P, CHUNK, PACK], BF16, name=f"x_bf{c}", align_bytes=64) for c in range(n_chunks)]
        x_codes = [keep.tile([P, HALF], U32, name=f"x_codes{h}", align_bytes=64) for h in range(n_halves)]
        x_scales = [keep.tile([P, HALF], U8, name=f"x_scales{h}", align_bytes=64) for h in range(n_halves)]
        wk_bf = [keep.tile([P, 2 * P, PACK], BF16, name="wk_bf0", align_bytes=64)]
        wk_codes = [keep.tile([P, 2 * P], U32, name=f"wk_codes{u}", align_bytes=64) for u in range(2)]
        wk_scales = [keep.tile([P, 2 * P], U8, name=f"wk_scales{u}", align_bytes=64) for u in range(2)]

        def gather(dst, i, j0, width):
            h, c0 = divmod(j0, HALF)
            listed = offsets[:, j0 // LIST_ROWS : (j0 + width) // LIST_ROWS]
            nc.vector.tensor_tensor(dst, planes[i][:].indirect(listed), weights[h][:, c0 : c0 + width], ALU.mult)

        def quantize_x(c):
            h, cc = divmod(c, chunks_per_half)
            cols = slice(cc * CHUNK, (cc + 1) * CHUNK)
            nc.vector.quantize_mx(
                out=x_codes[h][:, cols].bitcast(FP8X4),
                scales=x_scales[h][:, cols],
                in_=x_bf[c][:].rearrange("p j i -> p (j i)"),
            )

        def interleave_hi(c):
            h, cc = divmod(c, chunks_per_half)
            src = picked_hi[h][:, :, cc * CHUNK : (cc + 1) * CHUNK].rearrange("p i j -> p j i")
            if c == n_chunks - 1:
                nc.vector.tensor_copy(out=x_bf[c][:, :, 2:4], in_=src)
            else:
                nc.scalar.copy(out=x_bf[c][:, :, 2:4], in_=src)

        def round_wk(t):
            cols = slice((t % 2) * P, (t % 2 + 1) * P)
            dst = wk_bf[t // 2][:, cols, :].rearrange("p (n e) i -> p n i e", e=4)
            src = wk_raw[t // 2][:, :, cols].rearrange("p i (n e) -> p n i e", e=4)
            if t == 0:
                nc.vector.tensor_copy(out=dst, in_=src)
            else:
                nc.scalar.copy(out=dst, in_=src)

        def quantize_wk(t0, count):
            cols = slice((t0 % 2) * P, (t0 % 2 + count) * P)
            nc.vector.quantize_mx(
                out=wk_codes[t0 // 2][:, cols].bitcast(FP8X4),
                scales=wk_scales[t0 // 2][:, cols],
                in_=wk_bf[t0 // 2][:, cols, :].rearrange("p n i -> p (n i)"),
            )

        for i in range(2):
            for h in range(n_halves):
                gather(picked_lo[h][:, i, :], i, h * HALF, HALF)
        for c in range(n_chunks):
            h, cc = divmod(c, chunks_per_half)
            nc.scalar.copy(
                out=x_bf[c][:, :, 0:2],
                in_=picked_lo[h][:, :, cc * CHUNK : (cc + 1) * CHUNK].rearrange("p i j -> p j i"),
            )
        for h in range(n_halves):
            gather(picked_hi[h][:, 0, :], 2, h * HALF, HALF)
        for c in range(n_chunks):
            h, cc = divmod(c, chunks_per_half)
            gather(picked_hi[h][:, 1, cc * CHUNK : (cc + 1) * CHUNK], 3, c * CHUNK, CHUNK)
            if c < n_chunks - 1:
                interleave_hi(c)
        round_wk(0)
        round_wk(1)
        quantize_x(0)
        quantize_wk(0, 1)
        quantize_x(1)
        interleave_hi(n_chunks - 1)
        quantize_x(2)
        quantize_x(3)
        quantize_wk(1, 1)

        ve_banks = {}
        diffs = {}
        gates = {}

        def product(bank, codes, scales, h, width):
            for j0 in range(0, HALF, width):
                cols = slice(j0, j0 + width)
                nc.tensor.matmul_mx(
                    out=bank[:, cols],
                    lhsT=codes.bitcast(FP8X4),
                    lhsT_scale=scales,
                    rhs=x_codes[h][:, cols].bitcast(FP8X4),
                    rhs_scale=x_scales[h][:, cols],
                    start=True,
                    stop=True,
                )

        def carried(u):
            t, h = units[u]
            return res_first[h][:] if t == 0 else res_rest[t - 1][:, h * HALF : (h + 1) * HALF]

        def front(u):
            t, h = units[u]
            width = CHUNK if t == 0 else HALF
            rows = slice(t * P, (t + 1) * P)
            ve_banks[u] = ve_pool.tile([P, HALF], F32, name="ve_bank")
            product(ve_banks[u], wv_codes[:, rows], wv_plane[:, rows], h, width)
            ke_bank = ke_pool.tile([P, HALF], F32, name="ke_bank")
            pair_cols = slice((t % 2) * P, (t % 2 + 1) * P)
            product(ke_bank, wk_codes[t // 2][:, pair_cols], wk_scales[t // 2][:, pair_cols], h, width)
            gates[u] = keep.tile([P, HALF], F32, name=f"gate{u}")
            nc.scalar.activation(
                out=gates[u][:], in_=ke_bank[:], func=ACT.Sigmoid, bias=neg_bias[:, t : t + 1], scale=-1.0
            )
            diffs[u] = keep.tile([P, HALF], F32, name=f"diff{u}")
            nc.vector.scalar_tensor_tensor(
                out=diffs[u][:], in0=ve_banks[u][:], scalar=0.0, in1=carried(u), op0=ALU.max, op1=ALU.subtract
            )

        def middle(u):
            engine = nc.vector if u in (4, 6) else nc.gpsimd
            engine.tensor_tensor(out=gates[u][:], in0=gates[u][:], in1=diffs[u][:], op=ALU.mult)

        def back(u):
            t, h = units[u]
            width = CHUNK if u == len(units) - 1 else HALF
            result = carried(u + 2) if u + 2 < len(units) else diffs[u][:]
            for j0 in range(0, HALF, width):
                cols = slice(j0, j0 + width)
                nc.vector.scalar_tensor_tensor(
                    out=result[:, cols],
                    in0=ve_banks[u][:, cols],
                    scalar=0.0,
                    in1=gates[u][:, cols],
                    op0=ALU.max,
                    op1=ALU.subtract,
                )
                nc.sync.dma_start(
                    out=out[t * P : (t + 1) * P, h * HALF + j0 : h * HALF + j0 + width], in_=result[:, cols]
                )

        front(0)
        middle(0)
        front(1)
        middle(1)
        wk_bf.append(keep.tile([P, 2 * P, PACK], BF16, name="wk_bf1", tag="res0_1", align_bytes=64))
        round_wk(2)
        front(2)
        middle(2)
        back(0)
        round_wk(3)
        front(3)
        middle(3)
        back(1)
        quantize_wk(2, 2)
        for u in range(4, len(units)):
            front(u)
            middle(u)
            back(u - 2)
        back(len(units) - 2)
        back(len(units) - 1)
